import numpy as np
import ml_dtypes


def mxq(x, axis, fmt="e4m3"):
    dtype, down = {"e4m3": (ml_dtypes.float8_e4m3fn, 7), "e5m2": (ml_dtypes.float8_e5m2, 14)}[fmt]
    v = np.moveaxis(np.asarray(x, np.float32).astype(ml_dtypes.bfloat16).astype(np.float64), axis, -1)
    blocks = v.reshape(v.shape[:-1] + (-1, 32))
    amax = np.abs(blocks).max(-1, keepdims=True)
    byte = np.maximum(np.where(amax > 0, np.frexp(amax)[1] - 1 + 127, 0) - down, 1)
    scale = np.exp2(byte - 127.0)
    codes = (blocks / scale).astype(np.float32).astype(dtype).astype(np.float64)
    return np.moveaxis((codes * scale).reshape(v.shape), -1, axis)


WIDE = False


def mx_kscale(k):
    if not WIDE:
        return np.ones(k)
    levels = np.array([10, -10, 5, -5, 0])
    if k % 512:
        return np.exp2(np.random.permutation(np.resize(levels, k // 32))).repeat(32)
    a = np.empty((k // 512, 16))
    for p in range(k // 512):
        a[p, :8] = np.random.permutation(np.resize(levels, 8))
        for g in range(8):
            far = levels[np.abs(levels - a[p, g]) >= 10]
            a[p, g + 8] = far[np.random.randint(len(far))]
    return np.exp2(a.ravel()).repeat(32)


def f64(x):
    return np.asarray(x).astype(np.float64)


def striped(idx):
    return np.tile(idx.reshape(-1, 16).T, (8, 1)).astype(np.uint16)


def unstriped(offs):
    return offs[:16].T.reshape(-1).astype(np.int64)


def striped8(idx):
    return np.concatenate([x.reshape(-1, 16).T for x in idx]).astype(np.uint16)


def runs(offs, k):
    lists = np.stack([offs[16 * r : 16 * r + 16].T.reshape(-1) for r in range(8)]).astype(np.int64)
    return lists[np.arange(k) % 512 // 64]


def pack_weight(w):
    k, n = w.shape
    w = f64(np.asarray(w, np.float32).astype(ml_dtypes.bfloat16)).reshape(k // 32, 32, n)
    amax = np.abs(w).max(1)
    byte = np.clip(np.where(amax > 0, np.frexp(amax)[1] - 1 + 127 - 7, 1), 1, 254)
    scaled = (w * np.exp2(127.0 - byte)[:, None, :]).reshape(k, n).astype(np.float32)
    words = np.ascontiguousarray(scaled.reshape(k // 512, 128, 4, n).transpose(0, 1, 3, 2)).astype(ml_dtypes.float8_e4m3fn).view(np.uint8)
    return words, np.ascontiguousarray(byte.astype(np.uint8).reshape(k // 512, 16, n))


def unpack_weight(words, scales):
    g, p, n, _ = words.shape
    vals = np.ascontiguousarray(words).view(ml_dtypes.float8_e4m3fn).astype(np.float64) * np.repeat(np.exp2(scales.astype(np.float64) - 127.0), 8, axis=1)[..., None]
    return vals.transpose(0, 1, 3, 2).reshape(g * 512, n)

def planes(y):
    n, m = y.shape
    v = y.astype(np.float32).astype(ml_dtypes.bfloat16).astype(np.float64).reshape(n // 32, 32, m)
    top = np.abs(v).max(1)
    byte = np.clip(np.where(top > 0, np.frexp(top)[1] - 1 + 127 - 7, 1), 1, 254)
    codes = (v * np.exp2(127.0 - byte)[:, None, :]).reshape(n, m).astype(np.float32).astype(ml_dtypes.float8_e4m3fn).view(np.uint8)
    words = codes.reshape(n // 512, 128, 4, m).transpose(0, 1, 3, 2)
    return np.ascontiguousarray(words), np.ascontiguousarray(byte.astype(np.uint8).reshape(n // 512, 16, m))


K, T, S, G, H = 512, 1024, 512, 2048, 512


def setup_inputs():
    n = np.random.standard_normal
    s = mx_kscale(K)[:, None]
    packed_xT = pack_weight(n((K, T)) * s)
    packed_dT = pack_weight(n((K, G)) / s)
    return {
        "x_words": packed_xT[0],
        "x_scales": packed_xT[1],
        "d_words": packed_dT[0],
        "d_scales": packed_dT[1],
        "gs": (np.random.uniform(0.5, 1.5, (K, 1)) * s).astype(np.float32),
        "offs": striped(np.random.permutation(T)[:S]),
        "k1": striped8(np.random.randint(0, G, (8, H))),
        "n1": striped(np.random.permutation(S)),
        "n2": striped(np.random.permutation(S)),
        "n3": striped(np.random.permutation(S)),
        "k2": striped8(np.random.randint(0, G, (8, H))),
        "n4": striped(np.random.permutation(S)),
        "n5": striped(np.random.permutation(S)),
    }


def reference(x_words, x_scales, d_words, d_scales, gs, offs, k1, n1, n2, n3, k2, n4, n5):
    d_k2 = unpack_weight(d_words, d_scales)[np.arange(K)[:, None], runs(k2, K)]
    d_k1 = unpack_weight(d_words, d_scales)[np.arange(K)[:, None], runs(k1, K)]
    xq = unpack_weight(x_words, x_scales)[:, unstriped(offs)]
    h = 0.0625 * (d_k1.T @ xq)
    z = f64(gs) * (h + h[:, unstriped(n1)] - (np.maximum(h[:, unstriped(n2)], h[:, unstriped(n3)])))
    h2 = 0.0625 * ((d_k2.T @ mxq(z, 0, "e4m3")))
    st = np.maximum(h2, h2[:, unstriped(n4)])
    out_0 = st[:, unstriped(n5)] - (0.5 * h2)
    return (out_0,) + planes(out_0)

@@ -1,0 +1,238 @@
+from contextlib import ExitStack
+
+import concourse.mybir as mybir
+from concourse.masks import make_identity
+
+K, T, S, G, H = 512, 1024, 512, 2048, 512
+FLOPS = 2 * 2 * K * H * S
+
+F32 = mybir.dt.float32
+BF16 = mybir.dt.bfloat16
+I32 = mybir.dt.int32
+U32 = mybir.dt.uint32
+U16 = mybir.dt.uint16
+U8 = mybir.dt.uint8
+FP8X4 = mybir.dt.float8_e4m3fn_x4
+ALU = mybir.AluOpType
+COPY = mybir.ActivationFunctionType.Copy
+
+P = 128
+TILES = 4
+HALF = S // 2
+HALF_COLS = HALF // 16
+SIXTEENTH = 0.0625
+CHUNKS = ((0, 256), (256, 256))
+H_ON_VECTOR = ()
+N2_ON_SCALAR = ()
+N4_ON_SCALAR = ((0, 0), (1, 0), (2, 0), (2, 1), (3, 0))
+OUT_CHUNKS = ((0, 256), (256, 128), (384, 128))
+
+
+def tile_picked_codetrimhopb_none_po_kernel(
+    tc, x_words, x_scales, d_words, d_scales, gs, offs, k1, n1, n2, n3, k2, n4, n5, out_0, out_1, out_2
+):
+    nc = tc.nc
+    with ExitStack() as ctx:
+        lists = ctx.enter_context(tc.tile_pool(name="lists", bufs=1))
+        sb = ctx.enter_context(tc.tile_pool(name="sb", bufs=1))
+        ring = ctx.enter_context(tc.tile_pool(name="ring", bufs=2))
+        ps = ctx.enter_context(tc.psum_pool(name="ps", bufs=1))
+
+        def load_list(name, src):
+            tile = lists.tile([P, S // 16], U16, name=name)
+            nc.sync.dma_start(tile[:], src)
+            return tile
+
+        def part_of(offsets, lo, n):
+            return offsets[:, lo // 16 : (lo + n) // 16]
+
+        def sbuf(name, shape, dtype, tag=None):
+            return sb.tile(shape, dtype, name=name, tag=tag or name, align_bytes=64)
+
+        def bank(index, shape):
+            return ps.tile(shape, F32, name=f"bank{index}")
+
+        k1_t = load_list("k1_t", k1)
+        x_bytes = sbuf("x_bytes", [P, T], U8)
+        x_rows = x_scales[0].bitcast(I32).rearrange("(q r) n -> r q n", r=4)
+        for r in range(4):
+            nc.scalar.dma_start(x_bytes[r:P:4, :].bitcast(I32), x_rows[r].unsqueeze(1).broadcast_to([4, 8, T // 4]))
+        d_bytes = sbuf("d_bytes", [P, G], U8)
+        nc.sync.dma_start(d_bytes[:].bitcast(I32), d_scales[0].bitcast(I32).unsqueeze(1).broadcast_to([16, 8, G // 4]))
+        offs_t = load_list("offs_t", offs)
+        x_tab = sbuf("x_tab", [P, T], U32)
+        nc.sync.dma_start(x_tab[:].bitcast(I32), x_words[0].rearrange("p n t -> p (n t)").bitcast(I32))
+        n3_t = load_list("n3_t", n3)
+        n1_t = load_list("n1_t", n1)
+        gs_col = sbuf("gs_col", [P, TILES], F32)
+        nc.sync.dma_start(gs_col[:], gs.rearrange("(p t) o -> p (t o)", t=TILES))
+        d_tab = sbuf("d_tab", [P, G], U32)
+        nc.sync.dma_start(d_tab[:].bitcast(I32), d_words[0].rearrange("p n t -> p (n t)").bitcast(I32))
+        n2_t = load_list("n2_t", n2)
+        k2_t = load_list("k2_t", k2)
+        n4_t = load_list("n4_t", n4)
+        n5_t = load_list("n5_t", n5)
+        ident = sbuf("ident", [P, P], F32)
+        make_identity(nc, ident[:])
+
+        def place_scale_rows(name, rows):
+            plane = sbuf(name, [P, H], U8)
+            nc.vector.tensor_copy(plane[:].bitcast(I32), rows[:].bitcast(I32))
+            for r in range(1, 4):
+                nc.sync.dma_start(plane[r:P:32, :].bitcast(I32), rows[8 * r : P : 32, :].bitcast(I32))
+            return plane
+
+        k1_rows = sbuf("k1_rows", [P, H], U8)
+        nc.vector.tensor_copy(k1_rows[:], d_bytes[:].indirect(k1_t[:]))
+        k1_plane = place_scale_rows("k1_plane", k1_rows)
+        xq_words = sbuf("xq_words", [P, S], U32)
+        nc.vector.tensor_copy(xq_words[:], x_tab[:].indirect(offs_t[:]))
+        xq_plane = sbuf("xq_plane", [P, S], U8)
+        nc.vector.tensor_copy(xq_plane[:], x_bytes[:].indirect(offs_t[:]))
+        k1_words = []
+        for hf in range(2):
+            w = sbuf(f"k1_words{hf}", [P, HALF], U32)
+            nc.vector.tensor_copy(w[:], d_tab[:].indirect(part_of(k1_t, hf * HALF, HALF)))
+            k1_words.append(w)
+
+        gs_bank = bank(7, [P, TILES, P])
+        for t in range(TILES):
+            nc.tensor.matmul(gs_bank[:, t, :], gs_col[:, t : t + 1].to_broadcast([P, P]), ident[:], start=True, stop=True, is_transpose=True)
+        gs_row = sbuf("gs_row", [P, 2, P, 2], F32)
+        nc.scalar.copy(gs_row[:], gs_bank[:].rearrange("k (u e) p -> k u p e", u=2))
+
+        h = []
+        for t in range(TILES):
+            acc = bank(t, [P, S])
+            cols = slice((t % 2) * P, (t % 2 + 1) * P)
+            nc.tensor.matmul_mx(
+                out=acc[:], lhsT=k1_words[t // 2][:, cols].bitcast(FP8X4), lhsT_scale=k1_plane[:, t * P : (t + 1) * P],
+                rhs=xq_words[:].bitcast(FP8X4), rhs_scale=xq_plane[:], start=True, stop=True,
+            )
+            h.append((acc, sbuf(f"h{t}", [P, S], F32)))
+
+        z_banks = [bank(4 + b, [P, H]) for b in range(4)]
+        h2_banks = []
+        h2 = [sbuf(f"h2_{t}", [P, S], F32) for t in range(TILES)]
+        k2_ops = []
+
+        def neighbours(t, c, m_tag=None):
+            lo, n = CHUNKS[c]
+            acc, win = h[t]
+            if c == 0:
+                if t in H_ON_VECTOR:
+                    nc.vector.tensor_scalar_mul(win[:], acc[:], SIXTEENTH)
+                else:
+                    nc.scalar.activation(win[:], acc[:], COPY, scale=SIXTEENTH)
+            g3 = ring.tile([P, n], F32, name=f"g3_{t}_{c}", tag="g3")
+            nc.scalar.activation(g3[:], win[:].indirect(part_of(n3_t, lo, n)), COPY, scale=-1.0)
+            g2 = ring.tile([P, n], F32, name=f"g2_{t}_{c}", tag="g2")
+            if (t, c) in N2_ON_SCALAR:
+                nc.scalar.activation(g2[:], win[:].indirect(part_of(n2_t, lo, n)), COPY)
+            else:
+                nc.vector.tensor_copy(g2[:], win[:].indirect(part_of(n2_t, lo, n)))
+            g1 = ring.tile([P, n], F32, name=f"g1_{t}_{c}", tag="g1")
+            nc.scalar.activation(g1[:], win[:].indirect(part_of(n1_t, lo, n)), COPY)
+            m = sbuf(f"m_{t}_{c}", [P, n], F32, m_tag)
+            nc.vector.scalar_tensor_tensor(m[:], g2[:], -1.0, g3[:], ALU.mult, ALU.min)
+            for bb in range(n // P):
+                b = lo // P + bb
+                dst = z_banks[b][:, t * P : (t + 1) * P]
+                terms = (win[:, b * P : (b + 1) * P], m[:, bb * P : (bb + 1) * P], g1[:, bb * P : (bb + 1) * P])
+                for i, term in enumerate(terms):
+                    nc.tensor.matmul(dst, term, ident[:], start=(i == 0), stop=(i == 2), is_transpose=True)
+
+        def second_operands():
+            rows = sbuf("k2_rows", [P, H], U8)
+            nc.vector.tensor_copy(rows[:], d_bytes[:].indirect(k2_t[:]))
+            dealt = sbuf("k2_rows_dealt", [P, H], U8)
+            nc.vector.tensor_copy(dealt[:].rearrange("p (t m) -> p t m", t=TILES), rows[:].rearrange("p (m t) -> p t m", t=TILES))
+            plane = place_scale_rows("k2_plane", dealt)
+            words = sbuf("k2_words", [P, H], U32)
+            nc.vector.tensor_copy(words[:], d_tab[:].indirect(k2_t[:]))
+            words_dealt = sbuf("k2_words_dealt", [P, H], U32)
+            nc.vector.tensor_copy(
+                words_dealt[:].bitcast(I32).rearrange("p (t m) -> p t m", t=TILES), words[:].bitcast(I32).rearrange("p (m t) -> p t m", t=TILES)
+            )
+            k2_ops.extend([words_dealt, plane])
+
+        def second_product(c):
+            lo, n = CHUNKS[c]
+            blocks = n // P
+            zt = []
+            for bb in range(blocks):
+                b = lo // P + bb
+                z = sbuf(f"zt{b}", [P, H], BF16)
+                nc.vector.tensor_tensor(
+                    z[:].rearrange("k (u p e) -> k u p e", u=2, e=2),
+                    z_banks[b][:].rearrange("k (p u e) -> k u p e", u=2, e=2), gs_row[:], ALU.mult,
+                )
+                zt.append(z)
+            back = bank(4 + lo // P, [P, blocks, 2, P])
+            for bb in range(blocks):
+                for u in range(2):
+                    nc.tensor.transpose(back[:, bb, u, :], zt[bb][:].bitcast(F32)[:, u * P : (u + 1) * P], ident[:])
+            zb = sbuf(f"zb{c}", [P, n * 4], BF16)
+            nc.scalar.copy(zb[:].bitcast(F32).rearrange("p (b r u) -> p b r u", b=blocks, u=2), back[:].rearrange("p b u r -> p b r u"))
+            codes = sbuf(f"z_codes{c}", [P, n], U32)
+            plane = sbuf(f"z_plane{c}", [P, n], U8)
+            nc.vector.quantize_mx(out=codes[:].bitcast(FP8X4), scales=plane[:], in_=zb[:])
+            for t in range(TILES):
+                if c == 0:
+                    h2_banks.append(bank(t, [P, S]))
+                cols = slice(lo, lo + n)
+                nc.tensor.matmul_mx(
+                    out=h2_banks[t][:, cols], lhsT=k2_ops[0][:, t * P : (t + 1) * P].bitcast(FP8X4),
+                    lhsT_scale=k2_ops[1][:, t * P : (t + 1) * P], rhs=codes[:].bitcast(FP8X4), rhs_scale=plane[:],
+                    start=True, stop=True,
+                )
+                if c == 1 and t % 2 == 1:
+                    nc.vector.tensor_scalar_mul(h2[t][:, cols], h2_banks[t][:, cols], SIXTEENTH)
+                else:
+                    nc.scalar.activation(h2[t][:, cols], h2_banks[t][:, cols], COPY, scale=SIXTEENTH)
+
+        neighbours(0, 0)
+        second_operands()
+        for t in range(1, TILES):
+            neighbours(t, 0)
+        neighbours(0, 1)
+        second_product(0)
+        neighbours(1, 1, m_tag="zt0")
+        neighbours(2, 1)
+        neighbours(3, 1)
+        second_product(1)
+
+        y = [sbuf(f"y{c}", [P, TILES, n], F32) for c, (lo, n) in enumerate(OUT_CHUNKS)]
+        out_rows = out_0.rearrange("(p t) j -> p t j", t=TILES)
+        st = []
+        for t in range(TILES):
+            st.append(sbuf(f"st{t}", [P, S], F32))
+            g4 = sbuf(f"g4_{t}", [P, S], F32)
+            for hf in range(2):
+                cols = slice(hf * HALF, (hf + 1) * HALF)
+                if (t, hf) in N4_ON_SCALAR:
+                    nc.scalar.activation(g4[:, cols], h2[t][:].indirect(part_of(n4_t, hf * HALF, HALF)), COPY)
+                else:
+                    nc.vector.tensor_copy(g4[:, cols], h2[t][:].indirect(part_of(n4_t, hf * HALF, HALF)))
+            nc.vector.tensor_tensor(st[t][:], g4[:], h2[t][:], ALU.max)
+
+        g5_halves = [sbuf("g5_first", [P, TILES, HALF], F32), sbuf("g5_second", [P, TILES, HALF], F32, tag="g4_3")]
+        y_codes = sbuf("y_codes", [P, S], U32)
+        y_plane = sbuf("y_plane", [P, S], U8)
+        out_words = out_1[0].rearrange("p n t -> p (n t)").bitcast(I32)
+        for c, (lo, n) in enumerate(OUT_CHUNKS):
+            cols = slice(lo, lo + n)
+            for t in range(TILES):
+                g5 = g5_halves[lo // HALF][:, t, lo % HALF : lo % HALF + n]
+                nc.scalar.activation(g5, st[t][:].indirect(part_of(n5_t, lo, n)), COPY)
+                nc.vector.scalar_tensor_tensor(y[c][:, t, :], h2[t][:, cols], -0.5, g5, ALU.mult, ALU.add)
+            nc.sync.dma_start(out_rows[:, :, cols], y[c][:])
+            yb = sbuf(f"yb{c}", [P, n * 4], BF16)
+            nc.vector.tensor_copy(
+                yb[:].rearrange("p (c i t) -> p c t i", i=4, t=TILES), y[c][:].rearrange("p t (c i) -> p c t i", i=4)
+            )
+            nc.vector.quantize_mx(out=y_codes[:, cols].bitcast(FP8X4), scales=y_plane[:, cols], in_=yb[:])
+            nc.sync.dma_start(out_words[:, cols], y_codes[:, cols].bitcast(I32))
+        for q in range(4):
+            eng = nc.sync if q % 2 == 0 else nc.scalar
+            eng.dma_start(out_2[0, 4 * q : 4 * q + 4, :].bitcast(I32), y_plane[32 * q : 32 * q + 4, :].bitcast(I32))

@@ -21,7 +21,10 @@ TILES = 4
 HALF = S // 2
 HALF_COLS = HALF // 16
 SIXTEENTH = 0.0625
-CHUNKS = ((0, 256), (256, 256))
+CHUNKS = ((0, 128), (128, 128), (256, 128), (384, 128))
+LAST = 3
+IL_ON_SCALAR = ()
+MT = 9
 H_ON_VECTOR = ()
 N2_ON_SCALAR = ()
 N4_ON_SCALAR = ((0, 0), (1, 0), (2, 0), (2, 1), (3, 0))
@@ -54,37 +57,39 @@ def tile_picked_codetrimhopb_none_po_kernel(
 
         k1_t = load_list("k1_t", k1)
         x_bytes = sbuf("x_bytes", [P, T], U8)
-        x_rows = x_scales[0].bitcast(I32).rearrange("(q r) n -> r q n", r=4)
-        for r in range(4):
-            nc.scalar.dma_start(x_bytes[r:P:4, :].bitcast(I32), x_rows[r].unsqueeze(1).broadcast_to([4, 8, T // 4]))
+        for q in range(4):
+            rows = x_scales[0, 4 * q : 4 * q + 4, :].bitcast(I32)
+            nc.scalar.dma_start(x_bytes[32 * q : 32 * q + 32, :].bitcast(I32), rows.partition_broadcast(8))
         d_bytes = sbuf("d_bytes", [P, G], U8)
         nc.sync.dma_start(d_bytes[:].bitcast(I32), d_scales[0].bitcast(I32).unsqueeze(1).broadcast_to([16, 8, G // 4]))
         offs_t = load_list("offs_t", offs)
         x_tab = sbuf("x_tab", [P, T], U32)
         nc.sync.dma_start(x_tab[:].bitcast(I32), x_words[0].rearrange("p n t -> p (n t)").bitcast(I32))
-        n3_t = load_list("n3_t", n3)
-        n1_t = load_list("n1_t", n1)
-        gs_col = sbuf("gs_col", [P, TILES], F32)
-        nc.sync.dma_start(gs_col[:], gs.rearrange("(p t) o -> p (t o)", t=TILES))
         d_tab = sbuf("d_tab", [P, G], U32)
-        nc.sync.dma_start(d_tab[:].bitcast(I32), d_words[0].rearrange("p n t -> p (n t)").bitcast(I32))
-        n2_t = load_list("n2_t", n2)
+        nc.scalar.dma_start(d_tab[:].bitcast(I32), d_words[0].rearrange("p n t -> p (n t)").bitcast(I32))
+        gs_col = sbuf("gs_col", [P, TILES], F32)
+        gs_rows = gs.rearrange("(p t) o -> p (t o)", t=TILES)
+        for lo in (0, P // 2):
+            nc.sync.dma_start(gs_col[lo : lo + P // 2, :], gs_rows[lo : lo + P // 2, :])
+        n3_t = load_list("n3_t", n3)
         k2_t = load_list("k2_t", k2)
+        n1_t = load_list("n1_t", n1)
+        n2_t = load_list("n2_t", n2)
         n4_t = load_list("n4_t", n4)
         n5_t = load_list("n5_t", n5)
         ident = sbuf("ident", [P, P], F32)
         make_identity(nc, ident[:])
 
-        def place_scale_rows(name, rows):
+        def place_scale_rows(name, rows, engine):
             plane = sbuf(name, [P, H], U8)
-            nc.vector.tensor_copy(plane[:].bitcast(I32), rows[:].bitcast(I32))
-            for r in range(1, 4):
-                nc.sync.dma_start(plane[r:P:32, :].bitcast(I32), rows[8 * r : P : 32, :].bitcast(I32))
+            nc.vector.memset(plane[:].bitcast(I32), 0)
+            for r in range(4):
+                engine.dma_start(plane[r:P:32, :].bitcast(I32), rows[8 * r : P : 32, :].bitcast(I32))
             return plane
 
         k1_rows = sbuf("k1_rows", [P, H], U8)
         nc.vector.tensor_copy(k1_rows[:], d_bytes[:].indirect(k1_t[:]))
-        k1_plane = place_scale_rows("k1_plane", k1_rows)
+        k1_plane = place_scale_rows("k1_plane", k1_rows, nc.scalar)
         xq_words = sbuf("xq_words", [P, S], U32)
         nc.vector.tensor_copy(xq_words[:], x_tab[:].indirect(offs_t[:]))
         xq_plane = sbuf("xq_plane", [P, S], U8)
@@ -147,60 +152,71 @@ def tile_picked_codetrimhopb_none_po_kernel(
             nc.vector.tensor_copy(rows[:], d_bytes[:].indirect(k2_t[:]))
             dealt = sbuf("k2_rows_dealt", [P, H], U8)
             nc.vector.tensor_copy(dealt[:].rearrange("p (t m) -> p t m", t=TILES), rows[:].rearrange("p (m t) -> p t m", t=TILES))
-            plane = place_scale_rows("k2_plane", dealt)
+            plane = place_scale_rows("k2_plane", dealt, nc.sync)
             words = sbuf("k2_words", [P, H], U32)
             nc.vector.tensor_copy(words[:], d_tab[:].indirect(k2_t[:]))
             words_dealt = sbuf("k2_words_dealt", [P, H], U32)
             nc.vector.tensor_copy(
-                words_dealt[:].bitcast(I32).rearrange("p (t m) -> p t m", t=TILES), words[:].bitcast(I32).rearrange("p (m t) -> p t m", t=TILES)
+                words_dealt[:].bitcast(I32).rearrange("p (t c i) -> p c t i", t=TILES, i=4),
+                words[:].bitcast(I32).rearrange("p (c i t) -> p c t i", t=TILES, i=4),
             )
             k2_ops.extend([words_dealt, plane])
 
-        def second_product(c):
-            lo, n = CHUNKS[c]
-            blocks = n // P
-            zt = []
-            for bb in range(blocks):
-                b = lo // P + bb
-                z = sbuf(f"zt{b}", [P, H], BF16)
-                nc.vector.tensor_tensor(
-                    z[:].rearrange("k (u p e) -> k u p e", u=2, e=2),
-                    z_banks[b][:].rearrange("k (p u e) -> k u p e", u=2, e=2), gs_row[:], ALU.mult,
-                )
-                zt.append(z)
-            back = bank(4 + lo // P, [P, blocks, 2, P])
-            for bb in range(blocks):
-                for u in range(2):
-                    nc.tensor.transpose(back[:, bb, u, :], zt[bb][:].bitcast(F32)[:, u * P : (u + 1) * P], ident[:])
-            zb = sbuf(f"zb{c}", [P, n * 4], BF16)
-            nc.scalar.copy(zb[:].bitcast(F32).rearrange("p (b r u) -> p b r u", b=blocks, u=2), back[:].rearrange("p b u r -> p b r u"))
-            codes = sbuf(f"z_codes{c}", [P, n], U32)
-            plane = sbuf(f"z_plane{c}", [P, n], U8)
-            nc.vector.quantize_mx(out=codes[:].bitcast(FP8X4), scales=plane[:], in_=zb[:])
+        def weigh(b, first, last):
+            ps_ = slice(32 * first, 32 * last)
+            nc.vector.tensor_tensor(
+                zt[b][:].rearrange("k (u p e) -> k u p e", u=2, e=2)[:, :, ps_, :],
+                z_banks[b][:].rearrange("k (p u e) -> k u p e", u=2, e=2)[:, :, ps_, :], gs_row[:, :, ps_, :], ALU.mult,
+            )
+
+        def turn_back(b):
+            back = bank(4 + b, [P, 2, P])
+            for u in range(2):
+                nc.tensor.transpose(back[:, u, :], zt[b][:].bitcast(F32)[:, u * P : (u + 1) * P], ident[:])
+            zb[b] = sbuf(f"zb{b}", [P, P * 4], BF16)
+            dst = zb[b][:].bitcast(F32).rearrange("p (r u) -> p r u", u=2)
+            if b == LAST:
+                nc.vector.tensor_copy(dst, back[:].rearrange("p u r -> p r u"))
+            else:
+                nc.scalar.copy(dst, back[:].rearrange("p u r -> p r u"))
+
+        def second_product(b):
+            codes = sbuf(f"z_codes{b}", [P, P], U32)
+            plane = sbuf(f"z_plane{b}", [P, P], U8)
+            nc.vector.quantize_mx(out=codes[:].bitcast(FP8X4), scales=plane[:], in_=zb[b][:])
             for t in range(TILES):
-                if c == 0:
+                if b == 0:
                     h2_banks.append(bank(t, [P, S]))
-                cols = slice(lo, lo + n)
                 nc.tensor.matmul_mx(
-                    out=h2_banks[t][:, cols], lhsT=k2_ops[0][:, t * P : (t + 1) * P].bitcast(FP8X4),
+                    out=h2_banks[t][:, b * P : (b + 1) * P], lhsT=k2_ops[0][:, t * P : (t + 1) * P].bitcast(FP8X4),
                     lhsT_scale=k2_ops[1][:, t * P : (t + 1) * P], rhs=codes[:].bitcast(FP8X4), rhs_scale=plane[:],
                     start=True, stop=True,
                 )
-                if c == 1 and t % 2 == 1:
-                    nc.vector.tensor_scalar_mul(h2[t][:, cols], h2_banks[t][:, cols], SIXTEENTH)
-                else:
-                    nc.scalar.activation(h2[t][:, cols], h2_banks[t][:, cols], COPY, scale=SIXTEENTH)
+                if b >= LAST - 1:
+                    cols = slice(LAST * P, S) if b == LAST else slice(0, LAST * P)
+                    if b == LAST and t % 2 == 1:
+                        nc.vector.tensor_scalar_mul(h2[t][:, cols], h2_banks[t][:, cols], SIXTEENTH)
+                    else:
+                        nc.scalar.activation(h2[t][:, cols], h2_banks[t][:, cols], COPY, scale=SIXTEENTH)
 
-        neighbours(0, 0)
-        second_operands()
-        for t in range(1, TILES):
-            neighbours(t, 0)
-        neighbours(0, 1)
-        second_product(0)
-        neighbours(1, 1, m_tag="zt0")
-        neighbours(2, 1)
-        neighbours(3, 1)
-        second_product(1)
+        zt, zb = {}, {}
+        for b in range(4):
+            for t in range(TILES):
+                neighbours(t, b, m_tag=(f"zt{b - 1}" if (b > 0 and t == MT) else None))
+                if b == 0 and t == 0:
+                    second_operands()
+                if b > 0 and t == 0:
+                    zt[b - 1] = sbuf(f"zt{b - 1}", [P, H], BF16)
+                    weigh(b - 1, 0, 4)
+                    turn_back(b - 1)
+                if b > 0 and t == 2:
+                    second_product(b - 1)
+                if b == LAST and t == 2:
+                    zt[b] = sbuf(f"zt{b}", [P, H], BF16)
+                    weigh(b, 0, 3)
+        weigh(LAST, 3, 4)
+        turn_back(LAST)
+        second_product(LAST)
 
         y = [sbuf(f"y{c}", [P, TILES, n], F32) for c, (lo, n) in enumerate(OUT_CHUNKS)]
         out_rows = out_0.rearrange("(p t) j -> p t j", t=TILES)
@@ -228,7 +244,7 @@ def tile_picked_codetrimhopb_none_po_kernel(
                 nc.vector.scalar_tensor_tensor(y[c][:, t, :], h2[t][:, cols], -0.5, g5, ALU.mult, ALU.add)
             nc.sync.dma_start(out_rows[:, :, cols], y[c][:])
             yb = sbuf(f"yb{c}", [P, n * 4], BF16)
-            nc.vector.tensor_copy(
+            (nc.scalar.copy if c in IL_ON_SCALAR else nc.vector.tensor_copy)(
                 yb[:].rearrange("p (c i t) -> p c t i", i=4, t=TILES), y[c][:].rearrange("p t (c i) -> p c t i", i=4)
             )
             nc.vector.quantize_mx(out=y_codes[:, cols].bitcast(FP8X4), scales=y_plane[:, cols], in_=yb[:])

@@ -18,17 +18,10 @@ COPY = mybir.ActivationFunctionType.Copy
 
 P = 128
 TILES = 4
+LAST = TILES - 1
 HALF = S // 2
-HALF_COLS = HALF // 16
+PAIRS = 32
 SIXTEENTH = 0.0625
-CHUNKS = ((0, 128), (128, 128), (256, 128), (384, 128))
-LAST = 3
-IL_ON_SCALAR = ()
-MT = 9
-H_ON_VECTOR = ()
-N2_ON_SCALAR = ()
-N4_ON_SCALAR = ((0, 0), (1, 0), (2, 0), (2, 1), (3, 0))
-OUT_CHUNKS = ((0, 256), (256, 128), (384, 128))
 
 
 def tile_picked_codetrimhopb_none_po_kernel(
@@ -46,8 +39,8 @@ def tile_picked_codetrimhopb_none_po_kernel(
             nc.sync.dma_start(tile[:], src)
             return tile
 
-        def part_of(offsets, lo, n):
-            return offsets[:, lo // 16 : (lo + n) // 16]
+        def half_of(offsets, hf):
+            return offsets[:, hf * HALF // 16 : (hf + 1) * HALF // 16]
 
         def sbuf(name, shape, dtype, tag=None):
             return sb.tile(shape, dtype, name=name, tag=tag or name, align_bytes=64)
@@ -55,104 +48,109 @@ def tile_picked_codetrimhopb_none_po_kernel(
         def bank(index, shape):
             return ps.tile(shape, F32, name=f"bank{index}")
 
+        def cols_of(index, width):
+            return slice(index * width, (index + 1) * width)
+
         k1_t = load_list("k1_t", k1)
         x_bytes = sbuf("x_bytes", [P, T], U8)
         for q in range(4):
             rows = x_scales[0, 4 * q : 4 * q + 4, :].bitcast(I32)
             nc.scalar.dma_start(x_bytes[32 * q : 32 * q + 32, :].bitcast(I32), rows.partition_broadcast(8))
+        offs_t = load_list("offs_t", offs)
         d_bytes = sbuf("d_bytes", [P, G], U8)
         nc.sync.dma_start(d_bytes[:].bitcast(I32), d_scales[0].bitcast(I32).unsqueeze(1).broadcast_to([16, 8, G // 4]))
-        offs_t = load_list("offs_t", offs)
         x_tab = sbuf("x_tab", [P, T], U32)
-        nc.sync.dma_start(x_tab[:].bitcast(I32), x_words[0].rearrange("p n t -> p (n t)").bitcast(I32))
-        d_tab = sbuf("d_tab", [P, G], U32)
-        nc.scalar.dma_start(d_tab[:].bitcast(I32), d_words[0].rearrange("p n t -> p (n t)").bitcast(I32))
-        gs_col = sbuf("gs_col", [P, TILES], F32)
-        gs_rows = gs.rearrange("(p t) o -> p (t o)", t=TILES)
-        for lo in (0, P // 2):
-            nc.sync.dma_start(gs_col[lo : lo + P // 2, :], gs_rows[lo : lo + P // 2, :])
+        nc.sync.dma_start(x_tab[:].bitcast(I32), x_words[0].rearrange("p n j -> p (n j)").bitcast(I32))
         n3_t = load_list("n3_t", n3)
-        k2_t = load_list("k2_t", k2)
         n1_t = load_list("n1_t", n1)
         n2_t = load_list("n2_t", n2)
+        d_tab = sbuf("d_tab", [P, G], U32)
+        nc.sync.dma_start(d_tab[:].bitcast(I32), d_words[0].rearrange("p n j -> p (n j)").bitcast(I32))
+        k2_t = load_list("k2_t", k2)
         n4_t = load_list("n4_t", n4)
         n5_t = load_list("n5_t", n5)
+        gs_col = sbuf("gs_col", [P, TILES], F32)
+        nc.gpsimd.dma_start(gs_col[:], gs.rearrange("(p j) o -> p (j o)", j=4))
         ident = sbuf("ident", [P, P], F32)
         make_identity(nc, ident[:])
 
-        def place_scale_rows(name, rows, engine):
+        def place_scale_rows(name, rows):
             plane = sbuf(name, [P, H], U8)
             nc.vector.memset(plane[:].bitcast(I32), 0)
             for r in range(4):
-                engine.dma_start(plane[r:P:32, :].bitcast(I32), rows[8 * r : P : 32, :].bitcast(I32))
+                nc.sync.dma_start(plane[r:P:32, :].bitcast(I32), rows[8 * r : P : 32, :].bitcast(I32))
             return plane
 
         k1_rows = sbuf("k1_rows", [P, H], U8)
         nc.vector.tensor_copy(k1_rows[:], d_bytes[:].indirect(k1_t[:]))
-        k1_plane = place_scale_rows("k1_plane", k1_rows, nc.scalar)
+        k1_plane = place_scale_rows("k1_plane", k1_rows)
         xq_words = sbuf("xq_words", [P, S], U32)
         nc.vector.tensor_copy(xq_words[:], x_tab[:].indirect(offs_t[:]))
         xq_plane = sbuf("xq_plane", [P, S], U8)
         nc.vector.tensor_copy(xq_plane[:], x_bytes[:].indirect(offs_t[:]))
         k1_words = []
         for hf in range(2):
-            w = sbuf(f"k1_words{hf}", [P, HALF], U32)
-            nc.vector.tensor_copy(w[:], d_tab[:].indirect(part_of(k1_t, hf * HALF, HALF)))
-            k1_words.append(w)
+            words = sbuf(f"k1_words{hf}", [P, HALF], U32)
+            nc.vector.tensor_copy(words[:], d_tab[:].indirect(half_of(k1_t, hf)))
+            k1_words.append(words)
 
         gs_bank = bank(7, [P, TILES, P])
-        for t in range(TILES):
-            nc.tensor.matmul(gs_bank[:, t, :], gs_col[:, t : t + 1].to_broadcast([P, P]), ident[:], start=True, stop=True, is_transpose=True)
+        for j in range(4):
+            nc.tensor.matmul(gs_bank[:, j, :], gs_col[:, j : j + 1].to_broadcast([P, P]), ident[:], start=True, stop=True, is_transpose=True)
         gs_row = sbuf("gs_row", [P, 2, P, 2], F32)
         nc.scalar.copy(gs_row[:], gs_bank[:].rearrange("k (u e) p -> k u p e", u=2))
 
-        h = []
+        h_banks = []
         for t in range(TILES):
             acc = bank(t, [P, S])
-            cols = slice((t % 2) * P, (t % 2 + 1) * P)
             nc.tensor.matmul_mx(
-                out=acc[:], lhsT=k1_words[t // 2][:, cols].bitcast(FP8X4), lhsT_scale=k1_plane[:, t * P : (t + 1) * P],
+                out=acc[:], lhsT=k1_words[t // 2][:, cols_of(t % 2, P)].bitcast(FP8X4), lhsT_scale=k1_plane[:, cols_of(t, P)],
                 rhs=xq_words[:].bitcast(FP8X4), rhs_scale=xq_plane[:], start=True, stop=True,
             )
-            h.append((acc, sbuf(f"h{t}", [P, S], F32)))
+            h_banks.append(acc)
+        h = [sbuf(f"h{t}", [P, S], F32) for t in range(TILES)]
 
-        z_banks = [bank(4 + b, [P, H]) for b in range(4)]
-        h2_banks = []
-        h2 = [sbuf(f"h2_{t}", [P, S], F32) for t in range(TILES)]
-        k2_ops = []
+        sums = [bank(4 + b, [P, H]) for b in range(4)]
+        sums_last = []
 
-        def neighbours(t, c, m_tag=None):
-            lo, n = CHUNKS[c]
-            acc, win = h[t]
-            if c == 0:
-                if t in H_ON_VECTOR:
-                    nc.vector.tensor_scalar_mul(win[:], acc[:], SIXTEENTH)
+        def add_turned(dst, term, start, stop):
+            nc.tensor.matmul(dst, term, ident[:], start=start, stop=stop, is_transpose=True)
+
+        def leave_first_product(t):
+            nc.scalar.activation(h[t][:], h_banks[t][:], COPY, scale=SIXTEENTH)
+            for b in range(2 if t == LAST else 4):
+                add_turned(sums[b][:, cols_of(t, P)], h[t][:, cols_of(b, P)], start=(t == 0), stop=False)
+
+        def open_sums_last():
+            sums_last.append(bank(5, [P, 2, P]))
+            for bb in range(2):
+                add_turned(sums_last[0][:, bb, :], h[LAST][:, cols_of(2 + bb, P)], start=(bb == 0), stop=False)
+
+        def neighbours(t, hf):
+            minus_n3 = ring.tile([P, HALF], F32, name="minus_n3")
+            nc.scalar.activation(minus_n3[:], h[t][:].indirect(half_of(n3_t, hf)), COPY, scale=-1.0)
+            at_n2 = ring.tile([P, HALF], F32, name="at_n2")
+            nc.vector.tensor_copy(at_n2[:], h[t][:].indirect(half_of(n2_t, hf)))
+            at_n1 = ring.tile([P, HALF], F32, name="at_n1")
+            nc.scalar.activation(at_n1[:], h[t][:].indirect(half_of(n1_t, hf)), COPY)
+            minus_max = sbuf(f"minus_max{t}_{hf}", [P, HALF], F32)
+            nc.vector.scalar_tensor_tensor(minus_max[:], at_n2[:], -1.0, minus_n3[:], ALU.mult, ALU.min)
+            for bb in range(2):
+                if hf == 1 and t == LAST:
+                    dst, closes = sums_last[0][:, bb, :], bb == 1
                 else:
-                    nc.scalar.activation(win[:], acc[:], COPY, scale=SIXTEENTH)
-            g3 = ring.tile([P, n], F32, name=f"g3_{t}_{c}", tag="g3")
-            nc.scalar.activation(g3[:], win[:].indirect(part_of(n3_t, lo, n)), COPY, scale=-1.0)
-            g2 = ring.tile([P, n], F32, name=f"g2_{t}_{c}", tag="g2")
-            if (t, c) in N2_ON_SCALAR:
-                nc.scalar.activation(g2[:], win[:].indirect(part_of(n2_t, lo, n)), COPY)
-            else:
-                nc.vector.tensor_copy(g2[:], win[:].indirect(part_of(n2_t, lo, n)))
-            g1 = ring.tile([P, n], F32, name=f"g1_{t}_{c}", tag="g1")
-            nc.scalar.activation(g1[:], win[:].indirect(part_of(n1_t, lo, n)), COPY)
-            m = sbuf(f"m_{t}_{c}", [P, n], F32, m_tag)
-            nc.vector.scalar_tensor_tensor(m[:], g2[:], -1.0, g3[:], ALU.mult, ALU.min)
-            for bb in range(n // P):
-                b = lo // P + bb
-                dst = z_banks[b][:, t * P : (t + 1) * P]
-                terms = (win[:, b * P : (b + 1) * P], m[:, bb * P : (bb + 1) * P], g1[:, bb * P : (bb + 1) * P])
-                for i, term in enumerate(terms):
-                    nc.tensor.matmul(dst, term, ident[:], start=(i == 0), stop=(i == 2), is_transpose=True)
+                    dst, closes = sums[2 * hf + bb][:, cols_of(t, P)], t == LAST - hf
+                add_turned(dst, minus_max[:, cols_of(bb, P)], start=False, stop=False)
+                add_turned(dst, at_n1[:, cols_of(bb, P)], start=False, stop=closes)
 
         def second_operands():
             rows = sbuf("k2_rows", [P, H], U8)
             nc.vector.tensor_copy(rows[:], d_bytes[:].indirect(k2_t[:]))
-            dealt = sbuf("k2_rows_dealt", [P, H], U8)
-            nc.vector.tensor_copy(dealt[:].rearrange("p (t m) -> p t m", t=TILES), rows[:].rearrange("p (m t) -> p t m", t=TILES))
-            plane = place_scale_rows("k2_plane", dealt, nc.sync)
+            rows_dealt = sbuf("k2_rows_dealt", [P, H], U8)
+            nc.vector.tensor_copy(
+                rows_dealt[:].rearrange("p (t m) -> p t m", t=TILES), rows[:].rearrange("p (m t) -> p t m", t=TILES)
+            )
+            plane = place_scale_rows("k2_plane", rows_dealt)
             words = sbuf("k2_words", [P, H], U32)
             nc.vector.tensor_copy(words[:], d_tab[:].indirect(k2_t[:]))
             words_dealt = sbuf("k2_words_dealt", [P, H], U32)
@@ -160,95 +158,98 @@ def tile_picked_codetrimhopb_none_po_kernel(
                 words_dealt[:].bitcast(I32).rearrange("p (t c i) -> p c t i", t=TILES, i=4),
                 words[:].bitcast(I32).rearrange("p (c i t) -> p c t i", t=TILES, i=4),
             )
-            k2_ops.extend([words_dealt, plane])
+            return words_dealt, plane
 
-        def weigh(b, first, last):
-            ps_ = slice(32 * first, 32 * last)
+        z_turned = [sbuf(f"z_turned{b}", [P, H], BF16) for b in range(4)]
+
+        def weigh(b, src, first_tile, tiles):
+            p_range = slice(PAIRS * first_tile, PAIRS * (first_tile + tiles))
             nc.vector.tensor_tensor(
-                zt[b][:].rearrange("k (u p e) -> k u p e", u=2, e=2)[:, :, ps_, :],
-                z_banks[b][:].rearrange("k (p u e) -> k u p e", u=2, e=2)[:, :, ps_, :], gs_row[:, :, ps_, :], ALU.mult,
+                z_turned[b][:].rearrange("k (u p e) -> k u p e", u=2, e=2)[:, :, p_range, :],
+                src.rearrange("k (p u e) -> k u p e", u=2, e=2), gs_row[:, :, p_range, :], ALU.mult,
             )
 
-        def turn_back(b):
-            back = bank(4 + b, [P, 2, P])
+        def turn_back(dst, b):
             for u in range(2):
-                nc.tensor.transpose(back[:, u, :], zt[b][:].bitcast(F32)[:, u * P : (u + 1) * P], ident[:])
-            zb[b] = sbuf(f"zb{b}", [P, P * 4], BF16)
-            dst = zb[b][:].bitcast(F32).rearrange("p (r u) -> p r u", u=2)
-            if b == LAST:
-                nc.vector.tensor_copy(dst, back[:].rearrange("p u r -> p r u"))
-            else:
-                nc.scalar.copy(dst, back[:].rearrange("p u r -> p r u"))
+                nc.tensor.transpose(dst[:, u, :], z_turned[b][:].bitcast(F32)[:, cols_of(u, P)], ident[:])
 
-        def second_product(b):
-            codes = sbuf(f"z_codes{b}", [P, P], U32)
-            plane = sbuf(f"z_plane{b}", [P, P], U8)
-            nc.vector.quantize_mx(out=codes[:].bitcast(FP8X4), scales=plane[:], in_=zb[b][:])
+        z_half = [sbuf(f"z_half{hf}", [P, HALF * 4], BF16) for hf in range(2)]
+        z_words = [z[:].bitcast(F32).rearrange("p (b c u) -> p b c u", b=2, u=2) for z in z_half]
+        h2_banks = []
+        h2 = [sbuf(f"h2_{t}", [P, S], F32) for t in range(TILES)]
+
+        def second_product(hf):
+            codes = sbuf(f"z_codes{hf}", [P, HALF], U32)
+            plane = sbuf(f"z_plane{hf}", [P, HALF], U8)
+            nc.vector.quantize_mx(out=codes[:].bitcast(FP8X4), scales=plane[:], in_=z_half[hf][:])
+            cols = cols_of(hf, HALF)
             for t in range(TILES):
-                if b == 0:
+                if hf == 0:
                     h2_banks.append(bank(t, [P, S]))
                 nc.tensor.matmul_mx(
-                    out=h2_banks[t][:, b * P : (b + 1) * P], lhsT=k2_ops[0][:, t * P : (t + 1) * P].bitcast(FP8X4),
-                    lhsT_scale=k2_ops[1][:, t * P : (t + 1) * P], rhs=codes[:].bitcast(FP8X4), rhs_scale=plane[:],
-                    start=True, stop=True,
+                    out=h2_banks[t][:, cols], lhsT=k2_words[:, cols_of(t, P)].bitcast(FP8X4), lhsT_scale=k2_plane[:, cols_of(t, P)],
+                    rhs=codes[:].bitcast(FP8X4), rhs_scale=plane[:], start=True, stop=True,
                 )
-                if b >= LAST - 1:
-                    cols = slice(LAST * P, S) if b == LAST else slice(0, LAST * P)
-                    if b == LAST and t % 2 == 1:
-                        nc.vector.tensor_scalar_mul(h2[t][:, cols], h2_banks[t][:, cols], SIXTEENTH)
-                    else:
-                        nc.scalar.activation(h2[t][:, cols], h2_banks[t][:, cols], COPY, scale=SIXTEENTH)
+                if hf == 1 and t % 2 == 1:
+                    nc.vector.tensor_scalar_mul(h2[t][:, cols], h2_banks[t][:, cols], SIXTEENTH)
+                else:
+                    nc.scalar.activation(h2[t][:, cols], h2_banks[t][:, cols], COPY, scale=SIXTEENTH)
 
-        zt, zb = {}, {}
-        for b in range(4):
-            for t in range(TILES):
-                neighbours(t, b, m_tag=(f"zt{b - 1}" if (b > 0 and t == MT) else None))
-                if b == 0 and t == 0:
-                    second_operands()
-                if b > 0 and t == 0:
-                    zt[b - 1] = sbuf(f"zt{b - 1}", [P, H], BF16)
-                    weigh(b - 1, 0, 4)
-                    turn_back(b - 1)
-                if b > 0 and t == 2:
-                    second_product(b - 1)
-                if b == LAST and t == 2:
-                    zt[b] = sbuf(f"zt{b}", [P, H], BF16)
-                    weigh(b, 0, 3)
-        weigh(LAST, 3, 4)
-        turn_back(LAST)
-        second_product(LAST)
+        leave_first_product(0)
+        neighbours(0, 0)
+        k2_words, k2_plane = second_operands()
+        for t in range(1, TILES):
+            leave_first_product(t)
+            neighbours(t, 0)
+        neighbours(0, 1)
+        for b in range(2):
+            weigh(b, sums[b][:], 0, TILES)
+        back = bank(4, [P, 2, 2, P])
+        for b in range(2):
+            turn_back(back[:, b], b)
+        nc.scalar.copy(z_words[0], back[:].rearrange("p b u c -> p b c u"))
+        open_sums_last()
+        neighbours(1, 1)
+        neighbours(2, 1)
+        second_product(0)
+        for b in range(2, 4):
+            weigh(b, sums[b][:, : LAST * P], 0, LAST)
+        neighbours(LAST, 1)
+        for bb in range(2):
+            weigh(2 + bb, sums_last[0][:, bb, :], LAST, 1)
+        for bb, copy in enumerate((nc.scalar.copy, nc.vector.tensor_copy)):
+            back = bank(6 + bb, [P, 2, P])
+            turn_back(back[:], 2 + bb)
+            copy(z_words[1][:, bb], back[:].rearrange("p u c -> p c u"))
+        second_product(1)
 
-        y = [sbuf(f"y{c}", [P, TILES, n], F32) for c, (lo, n) in enumerate(OUT_CHUNKS)]
-        out_rows = out_0.rearrange("(p t) j -> p t j", t=TILES)
         st = []
         for t in range(TILES):
+            at_n4 = sbuf(f"at_n4_{t}", [P, S], F32)
+            nc.scalar.activation(at_n4[:, :HALF], h2[t][:].indirect(half_of(n4_t, 0)), COPY)
+            nc.vector.tensor_copy(at_n4[:, HALF:], h2[t][:].indirect(half_of(n4_t, 1)))
             st.append(sbuf(f"st{t}", [P, S], F32))
-            g4 = sbuf(f"g4_{t}", [P, S], F32)
-            for hf in range(2):
-                cols = slice(hf * HALF, (hf + 1) * HALF)
-                if (t, hf) in N4_ON_SCALAR:
-                    nc.scalar.activation(g4[:, cols], h2[t][:].indirect(part_of(n4_t, hf * HALF, HALF)), COPY)
-                else:
-                    nc.vector.tensor_copy(g4[:, cols], h2[t][:].indirect(part_of(n4_t, hf * HALF, HALF)))
-            nc.vector.tensor_tensor(st[t][:], g4[:], h2[t][:], ALU.max)
+            nc.vector.tensor_tensor(st[t][:], at_n4[:], h2[t][:], ALU.max)
 
-        g5_halves = [sbuf("g5_first", [P, TILES, HALF], F32), sbuf("g5_second", [P, TILES, HALF], F32, tag="g4_3")]
+        at_n5 = [sbuf("at_n5_first", [P, TILES, HALF], F32), sbuf("at_n5_second", [P, TILES, HALF], F32, tag=f"at_n4_{LAST}")]
         y_codes = sbuf("y_codes", [P, S], U32)
         y_plane = sbuf("y_plane", [P, S], U8)
-        out_words = out_1[0].rearrange("p n t -> p (n t)").bitcast(I32)
-        for c, (lo, n) in enumerate(OUT_CHUNKS):
-            cols = slice(lo, lo + n)
+        out_rows = out_0.rearrange("(p t) j -> p t j", t=TILES)
+        out_words = out_1[0].rearrange("p n j -> p (n j)").bitcast(I32)
+        for hf in range(2):
+            cols = cols_of(hf, HALF)
+            y = sbuf(f"y{hf}", [P, TILES, HALF], F32)
             for t in range(TILES):
-                g5 = g5_halves[lo // HALF][:, t, lo % HALF : lo % HALF + n]
-                nc.scalar.activation(g5, st[t][:].indirect(part_of(n5_t, lo, n)), COPY)
-                nc.vector.scalar_tensor_tensor(y[c][:, t, :], h2[t][:, cols], -0.5, g5, ALU.mult, ALU.add)
-            nc.sync.dma_start(out_rows[:, :, cols], y[c][:])
-            yb = sbuf(f"yb{c}", [P, n * 4], BF16)
-            (nc.scalar.copy if c in IL_ON_SCALAR else nc.vector.tensor_copy)(
-                yb[:].rearrange("p (c i t) -> p c t i", i=4, t=TILES), y[c][:].rearrange("p t (c i) -> p c t i", i=4)
+                nc.scalar.activation(at_n5[hf][:, t, :], st[t][:].indirect(half_of(n5_t, hf)), COPY)
+                nc.vector.scalar_tensor_tensor(y[:, t, :], h2[t][:, cols], -0.5, at_n5[hf][:, t, :], ALU.mult, ALU.add)
+                if t % 2 == 1:
+                    nc.sync.dma_start(out_rows[:, t - 1 : t + 1, cols], y[:, t - 1 : t + 1, :])
+            y_half = sbuf(f"y_half{hf}", [P, HALF * 4], BF16)
+            nc.vector.tensor_copy(
+                y_half[:].rearrange("p (c i t) -> p c t i", i=4, t=TILES), y[:].rearrange("p t (c i) -> p c t i", i=4)
             )
-            nc.vector.quantize_mx(out=y_codes[:, cols].bitcast(FP8X4), scales=y_plane[:, cols], in_=yb[:])
+            nc.vector.quantize_mx(out=y_codes[:, cols].bitcast(FP8X4), scales=y_plane[:, cols], in_=y_half[:])
             nc.sync.dma_start(out_words[:, cols], y_codes[:, cols].bitcast(I32))
         for q in range(4):
-            eng = nc.sync if q % 2 == 0 else nc.scalar
-            eng.dma_start(out_2[0, 4 * q : 4 * q + 4, :].bitcast(I32), y_plane[32 * q : 32 * q + 4, :].bitcast(I32))
+            queue = nc.sync if q % 2 == 0 else nc.scalar
+            queue.dma_start(out_2[0, 4 * q : 4 * q + 4, :].bitcast(I32), y_plane[32 * q : 32 * q + 4, :].bitcast(I32))

@@ -117,7 +117,10 @@ def tile_picked_codetrimhopb_none_po_kernel(
             nc.tensor.matmul(dst, term, ident[:], start=start, stop=stop, is_transpose=True)
 
         def leave_first_product(t):
-            nc.scalar.activation(h[t][:], h_banks[t][:], COPY, scale=SIXTEENTH)
+            if t in (2,3):
+                nc.vector.tensor_scalar_mul(h[t][:], h_banks[t][:], SIXTEENTH)
+            else:
+                nc.scalar.activation(h[t][:], h_banks[t][:], COPY, scale=SIXTEENTH)
             for b in range(2 if t == LAST else 4):
                 add_turned(sums[b][:, cols_of(t, P)], h[t][:, cols_of(b, P)], start=(t == 0), stop=False)
 
@@ -127,11 +130,11 @@ def tile_picked_codetrimhopb_none_po_kernel(
                 add_turned(sums_last[0][:, bb, :], h[LAST][:, cols_of(2 + bb, P)], start=(bb == 0), stop=False)
 
         def neighbours(t, hf):
-            minus_n3 = ring.tile([P, HALF], F32, name="minus_n3")
+            minus_n3 = ring.tile([P, HALF], F32, name=f"minus_n3_{t}_{hf}", tag="minus_n3")
             nc.scalar.activation(minus_n3[:], h[t][:].indirect(half_of(n3_t, hf)), COPY, scale=-1.0)
-            at_n2 = ring.tile([P, HALF], F32, name="at_n2")
+            at_n2 = ring.tile([P, HALF], F32, name=f"at_n2_{t}_{hf}", tag="at_n2")
             nc.vector.tensor_copy(at_n2[:], h[t][:].indirect(half_of(n2_t, hf)))
-            at_n1 = ring.tile([P, HALF], F32, name="at_n1")
+            at_n1 = ring.tile([P, HALF], F32, name=f"at_n1_{t}_{hf}", tag="at_n1")
             nc.scalar.activation(at_n1[:], h[t][:].indirect(half_of(n1_t, hf)), COPY)
             minus_max = sbuf(f"minus_max{t}_{hf}", [P, HALF], F32)
             nc.vector.scalar_tensor_tensor(minus_max[:], at_n2[:], -1.0, minus_n3[:], ALU.mult, ALU.min)
@@ -151,14 +154,17 @@ def tile_picked_codetrimhopb_none_po_kernel(
                 rows_dealt[:].rearrange("p (t m) -> p t m", t=TILES), rows[:].rearrange("p (m t) -> p t m", t=TILES)
             )
             plane = place_scale_rows("k2_plane", rows_dealt)
-            words = sbuf("k2_words", [P, H], U32)
+            return plane
+
+        def second_words():
+            words = sbuf("k2_words", [P, H], U32, tag="h0")
             nc.vector.tensor_copy(words[:], d_tab[:].indirect(k2_t[:]))
             words_dealt = sbuf("k2_words_dealt", [P, H], U32)
             nc.vector.tensor_copy(
                 words_dealt[:].bitcast(I32).rearrange("p (t c i) -> p c t i", t=TILES, i=4),
                 words[:].bitcast(I32).rearrange("p (c i t) -> p c t i", t=TILES, i=4),
             )
-            return words_dealt, plane
+            return words_dealt
 
         z_turned = [sbuf(f"z_turned{b}", [P, H], BF16) for b in range(4)]
 
@@ -190,14 +196,11 @@ def tile_picked_codetrimhopb_none_po_kernel(
                     out=h2_banks[t][:, cols], lhsT=k2_words[:, cols_of(t, P)].bitcast(FP8X4), lhsT_scale=k2_plane[:, cols_of(t, P)],
                     rhs=codes[:].bitcast(FP8X4), rhs_scale=plane[:], start=True, stop=True,
                 )
-                if hf == 1 and t % 2 == 1:
-                    nc.vector.tensor_scalar_mul(h2[t][:, cols], h2_banks[t][:, cols], SIXTEENTH)
-                else:
-                    nc.scalar.activation(h2[t][:, cols], h2_banks[t][:, cols], COPY, scale=SIXTEENTH)
+                nc.scalar.activation(h2[t][:, cols], h2_banks[t][:, cols], COPY, scale=SIXTEENTH)
 
         leave_first_product(0)
         neighbours(0, 0)
-        k2_words, k2_plane = second_operands()
+        k2_plane = second_operands()
         for t in range(1, TILES):
             leave_first_product(t)
             neighbours(t, 0)
@@ -211,16 +214,17 @@ def tile_picked_codetrimhopb_none_po_kernel(
         open_sums_last()
         neighbours(1, 1)
         neighbours(2, 1)
-        second_product(0)
         for b in range(2, 4):
             weigh(b, sums[b][:, : LAST * P], 0, LAST)
         neighbours(LAST, 1)
+        k2_words = second_words()
         for bb in range(2):
             weigh(2 + bb, sums_last[0][:, bb, :], LAST, 1)
         for bb, copy in enumerate((nc.scalar.copy, nc.vector.tensor_copy)):
             back = bank(6 + bb, [P, 2, P])
             turn_back(back[:], 2 + bb)
             copy(z_words[1][:, bb], back[:].rearrange("p u c -> p c u"))
+        second_product(0)
         second_product(1)
 
         st = []

@@ -21,6 +21,7 @@ TILES = 4
 LAST = TILES - 1
 HALF = S // 2
 PAIRS = 32
+ON_VECTOR = 2
 SIXTEENTH = 0.0625
 
 
@@ -117,7 +118,7 @@ def tile_picked_codetrimhopb_none_po_kernel(
             nc.tensor.matmul(dst, term, ident[:], start=start, stop=stop, is_transpose=True)
 
         def leave_first_product(t):
-            if t in (2,3):
+            if t == ON_VECTOR:
                 nc.vector.tensor_scalar_mul(h[t][:], h_banks[t][:], SIXTEENTH)
             else:
                 nc.scalar.activation(h[t][:], h_banks[t][:], COPY, scale=SIXTEENTH)
@@ -146,15 +147,14 @@ def tile_picked_codetrimhopb_none_po_kernel(
                 add_turned(dst, minus_max[:, cols_of(bb, P)], start=False, stop=False)
                 add_turned(dst, at_n1[:, cols_of(bb, P)], start=False, stop=closes)
 
-        def second_operands():
+        def second_plane():
             rows = sbuf("k2_rows", [P, H], U8)
             nc.vector.tensor_copy(rows[:], d_bytes[:].indirect(k2_t[:]))
             rows_dealt = sbuf("k2_rows_dealt", [P, H], U8)
             nc.vector.tensor_copy(
                 rows_dealt[:].rearrange("p (t m) -> p t m", t=TILES), rows[:].rearrange("p (m t) -> p t m", t=TILES)
             )
-            plane = place_scale_rows("k2_plane", rows_dealt)
-            return plane
+            return place_scale_rows("k2_plane", rows_dealt)
 
         def second_words():
             words = sbuf("k2_words", [P, H], U32, tag="h0")
@@ -200,7 +200,7 @@ def tile_picked_codetrimhopb_none_po_kernel(
 
         leave_first_product(0)
         neighbours(0, 0)
-        k2_plane = second_operands()
+        k2_plane = second_plane()
         for t in range(1, TILES):
             leave_first_product(t)
             neighbours(t, 0)

from contextlib import ExitStack

import concourse.mybir as mybir
from concourse.masks import make_identity

K, T, S, G, H = 512, 1024, 512, 2048, 512
FLOPS = 2 * 2 * K * H * S

F32 = mybir.dt.float32
BF16 = mybir.dt.bfloat16
I32 = mybir.dt.int32
U32 = mybir.dt.uint32
U16 = mybir.dt.uint16
U8 = mybir.dt.uint8
FP8X4 = mybir.dt.float8_e4m3fn_x4
ALU = mybir.AluOpType
COPY = mybir.ActivationFunctionType.Copy

P = 128
TILES = 4
LAST = TILES - 1
HALF = S // 2
PAIRS = 32
ON_VECTOR = 2
SIXTEENTH = 0.0625


def tile_picked_codetrimhopb_none_po_kernel(
    tc, x_words, x_scales, d_words, d_scales, gs, offs, k1, n1, n2, n3, k2, n4, n5, out_0, out_1, out_2
):
    nc = tc.nc
    with ExitStack() as ctx:
        lists = ctx.enter_context(tc.tile_pool(name="lists", bufs=1))
        sb = ctx.enter_context(tc.tile_pool(name="sb", bufs=1))
        ring = ctx.enter_context(tc.tile_pool(name="ring", bufs=2))
        ps = ctx.enter_context(tc.psum_pool(name="ps", bufs=1))

        def load_list(name, src):
            tile = lists.tile([P, S // 16], U16, name=name)
            nc.sync.dma_start(tile[:], src)
            return tile

        def half_of(offsets, hf):
            return offsets[:, hf * HALF // 16 : (hf + 1) * HALF // 16]

        def sbuf(name, shape, dtype, tag=None):
            return sb.tile(shape, dtype, name=name, tag=tag or name, align_bytes=64)

        def bank(index, shape):
            return ps.tile(shape, F32, name=f"bank{index}")

        def cols_of(index, width):
            return slice(index * width, (index + 1) * width)

        k1_t = load_list("k1_t", k1)
        x_bytes = sbuf("x_bytes", [P, T], U8)
        for q in range(4):
            rows = x_scales[0, 4 * q : 4 * q + 4, :].bitcast(I32)
            nc.scalar.dma_start(x_bytes[32 * q : 32 * q + 32, :].bitcast(I32), rows.partition_broadcast(8))
        offs_t = load_list("offs_t", offs)
        d_bytes = sbuf("d_bytes", [P, G], U8)
        nc.sync.dma_start(d_bytes[:].bitcast(I32), d_scales[0].bitcast(I32).unsqueeze(1).broadcast_to([16, 8, G // 4]))
        x_tab = sbuf("x_tab", [P, T], U32)
        nc.sync.dma_start(x_tab[:].bitcast(I32), x_words[0].rearrange("p n j -> p (n j)").bitcast(I32))
        n3_t = load_list("n3_t", n3)
        n1_t = load_list("n1_t", n1)
        n2_t = load_list("n2_t", n2)
        d_tab = sbuf("d_tab", [P, G], U32)
        nc.sync.dma_start(d_tab[:].bitcast(I32), d_words[0].rearrange("p n j -> p (n j)").bitcast(I32))
        k2_t = load_list("k2_t", k2)
        n4_t = load_list("n4_t", n4)
        n5_t = load_list("n5_t", n5)
        gs_col = sbuf("gs_col", [P, TILES], F32)
        nc.gpsimd.dma_start(gs_col[:], gs.rearrange("(p j) o -> p (j o)", j=4))
        ident = sbuf("ident", [P, P], F32)
        make_identity(nc, ident[:])

        def place_scale_rows(name, rows):
            plane = sbuf(name, [P, H], U8)
            nc.vector.memset(plane[:].bitcast(I32), 0)
            for r in range(4):
                nc.sync.dma_start(plane[r:P:32, :].bitcast(I32), rows[8 * r : P : 32, :].bitcast(I32))
            return plane

        k1_rows = sbuf("k1_rows", [P, H], U8)
        nc.vector.tensor_copy(k1_rows[:], d_bytes[:].indirect(k1_t[:]))
        k1_plane = place_scale_rows("k1_plane", k1_rows)
        xq_words = sbuf("xq_words", [P, S], U32)
        nc.vector.tensor_copy(xq_words[:], x_tab[:].indirect(offs_t[:]))
        xq_plane = sbuf("xq_plane", [P, S], U8)
        nc.vector.tensor_copy(xq_plane[:], x_bytes[:].indirect(offs_t[:]))
        k1_words = []
        for hf in range(2):
            words = sbuf(f"k1_words{hf}", [P, HALF], U32)
            nc.vector.tensor_copy(words[:], d_tab[:].indirect(half_of(k1_t, hf)))
            k1_words.append(words)

        gs_bank = bank(7, [P, TILES, P])
        for j in range(4):
            nc.tensor.matmul(gs_bank[:, j, :], gs_col[:, j : j + 1].to_broadcast([P, P]), ident[:], start=True, stop=True, is_transpose=True)
        gs_row = sbuf("gs_row", [P, 2, P, 2], F32)
        nc.scalar.copy(gs_row[:], gs_bank[:].rearrange("k (u e) p -> k u p e", u=2))

        h_banks = []
        for t in range(TILES):
            acc = bank(t, [P, S])
            nc.tensor.matmul_mx(
                out=acc[:], lhsT=k1_words[t // 2][:, cols_of(t % 2, P)].bitcast(FP8X4), lhsT_scale=k1_plane[:, cols_of(t, P)],
                rhs=xq_words[:].bitcast(FP8X4), rhs_scale=xq_plane[:], start=True, stop=True,
            )
            h_banks.append(acc)
        h = [sbuf(f"h{t}", [P, S], F32) for t in range(TILES)]

        sums = [bank(4 + b, [P, H]) for b in range(4)]
        sums_last = []

        def add_turned(dst, term, start, stop):
            nc.tensor.matmul(dst, term, ident[:], start=start, stop=stop, is_transpose=True)

        def leave_first_product(t):
            if t == ON_VECTOR:
                nc.vector.tensor_scalar_mul(h[t][:], h_banks[t][:], SIXTEENTH)
            else:
                nc.scalar.activation(h[t][:], h_banks[t][:], COPY, scale=SIXTEENTH)
            for b in range(2 if t == LAST else 4):
                add_turned(sums[b][:, cols_of(t, P)], h[t][:, cols_of(b, P)], start=(t == 0), stop=False)

        def open_sums_last():
            sums_last.append(bank(5, [P, 2, P]))
            for bb in range(2):
                add_turned(sums_last[0][:, bb, :], h[LAST][:, cols_of(2 + bb, P)], start=(bb == 0), stop=False)

        def neighbours(t, hf):
            minus_n3 = ring.tile([P, HALF], F32, name=f"minus_n3_{t}_{hf}", tag="minus_n3")
            nc.scalar.activation(minus_n3[:], h[t][:].indirect(half_of(n3_t, hf)), COPY, scale=-1.0)
            at_n2 = ring.tile([P, HALF], F32, name=f"at_n2_{t}_{hf}", tag="at_n2")
            nc.vector.tensor_copy(at_n2[:], h[t][:].indirect(half_of(n2_t, hf)))
            at_n1 = ring.tile([P, HALF], F32, name=f"at_n1_{t}_{hf}", tag="at_n1")
            nc.scalar.activation(at_n1[:], h[t][:].indirect(half_of(n1_t, hf)), COPY)
            minus_max = sbuf(f"minus_max{t}_{hf}", [P, HALF], F32)
            nc.vector.scalar_tensor_tensor(minus_max[:], at_n2[:], -1.0, minus_n3[:], ALU.mult, ALU.min)
            for bb in range(2):
                if hf == 1 and t == LAST:
                    dst, closes = sums_last[0][:, bb, :], bb == 1
                else:
                    dst, closes = sums[2 * hf + bb][:, cols_of(t, P)], t == LAST - hf
                add_turned(dst, minus_max[:, cols_of(bb, P)], start=False, stop=False)
                add_turned(dst, at_n1[:, cols_of(bb, P)], start=False, stop=closes)

        def second_plane():
            rows = sbuf("k2_rows", [P, H], U8)
            nc.vector.tensor_copy(rows[:], d_bytes[:].indirect(k2_t[:]))
            rows_dealt = sbuf("k2_rows_dealt", [P, H], U8)
            nc.vector.tensor_copy(
                rows_dealt[:].rearrange("p (t m) -> p t m", t=TILES), rows[:].rearrange("p (m t) -> p t m", t=TILES)
            )
            return place_scale_rows("k2_plane", rows_dealt)

        def second_words():
            words = sbuf("k2_words", [P, H], U32, tag="h0")
            nc.vector.tensor_copy(words[:], d_tab[:].indirect(k2_t[:]))
            words_dealt = sbuf("k2_words_dealt", [P, H], U32)
            nc.vector.tensor_copy(
                words_dealt[:].bitcast(I32).rearrange("p (t c i) -> p c t i", t=TILES, i=4),
                words[:].bitcast(I32).rearrange("p (c i t) -> p c t i", t=TILES, i=4),
            )
            return words_dealt

        z_turned = [sbuf(f"z_turned{b}", [P, H], BF16) for b in range(4)]

        def weigh(b, src, first_tile, tiles):
            p_range = slice(PAIRS * first_tile, PAIRS * (first_tile + tiles))
            nc.vector.tensor_tensor(
                z_turned[b][:].rearrange("k (u p e) -> k u p e", u=2, e=2)[:, :, p_range, :],
                src.rearrange("k (p u e) -> k u p e", u=2, e=2), gs_row[:, :, p_range, :], ALU.mult,
            )

        def turn_back(dst, b):
            for u in range(2):
                nc.tensor.transpose(dst[:, u, :], z_turned[b][:].bitcast(F32)[:, cols_of(u, P)], ident[:])

        z_half = [sbuf(f"z_half{hf}", [P, HALF * 4], BF16) for hf in range(2)]
        z_words = [z[:].bitcast(F32).rearrange("p (b c u) -> p b c u", b=2, u=2) for z in z_half]
        h2_banks = []
        h2 = [sbuf(f"h2_{t}", [P, S], F32) for t in range(TILES)]

        def second_product(hf):
            codes = sbuf(f"z_codes{hf}", [P, HALF], U32)
            plane = sbuf(f"z_plane{hf}", [P, HALF], U8)
            nc.vector.quantize_mx(out=codes[:].bitcast(FP8X4), scales=plane[:], in_=z_half[hf][:])
            cols = cols_of(hf, HALF)
            for t in range(TILES):
                if hf == 0:
                    h2_banks.append(bank(t, [P, S]))
                nc.tensor.matmul_mx(
                    out=h2_banks[t][:, cols], lhsT=k2_words[:, cols_of(t, P)].bitcast(FP8X4), lhsT_scale=k2_plane[:, cols_of(t, P)],
                    rhs=codes[:].bitcast(FP8X4), rhs_scale=plane[:], start=True, stop=True,
                )
                nc.scalar.activation(h2[t][:, cols], h2_banks[t][:, cols], COPY, scale=SIXTEENTH)

        leave_first_product(0)
        neighbours(0, 0)
        k2_plane = second_plane()
        for t in range(1, TILES):
            leave_first_product(t)
            neighbours(t, 0)
        neighbours(0, 1)
        for b in range(2):
            weigh(b, sums[b][:], 0, TILES)
        back = bank(4, [P, 2, 2, P])
        for b in range(2):
            turn_back(back[:, b], b)
        nc.scalar.copy(z_words[0], back[:].rearrange("p b u c -> p b c u"))
        open_sums_last()
        neighbours(1, 1)
        neighbours(2, 1)
        for b in range(2, 4):
            weigh(b, sums[b][:, : LAST * P], 0, LAST)
        neighbours(LAST, 1)
        k2_words = second_words()
        for bb in range(2):
            weigh(2 + bb, sums_last[0][:, bb, :], LAST, 1)
        for bb, copy in enumerate((nc.scalar.copy, nc.vector.tensor_copy)):
            back = bank(6 + bb, [P, 2, P])
            turn_back(back[:], 2 + bb)
            copy(z_words[1][:, bb], back[:].rearrange("p u c -> p c u"))
        second_product(0)
        second_product(1)

        st = []
        for t in range(TILES):
            at_n4 = sbuf(f"at_n4_{t}", [P, S], F32)
            nc.scalar.activation(at_n4[:, :HALF], h2[t][:].indirect(half_of(n4_t, 0)), COPY)
            nc.vector.tensor_copy(at_n4[:, HALF:], h2[t][:].indirect(half_of(n4_t, 1)))
            st.append(sbuf(f"st{t}", [P, S], F32))
            nc.vector.tensor_tensor(st[t][:], at_n4[:], h2[t][:], ALU.max)

        at_n5 = [sbuf("at_n5_first", [P, TILES, HALF], F32), sbuf("at_n5_second", [P, TILES, HALF], F32, tag=f"at_n4_{LAST}")]
        y_codes = sbuf("y_codes", [P, S], U32)
        y_plane = sbuf("y_plane", [P, S], U8)
        out_rows = out_0.rearrange("(p t) j -> p t j", t=TILES)
        out_words = out_1[0].rearrange("p n j -> p (n j)").bitcast(I32)
        for hf in range(2):
            cols = cols_of(hf, HALF)
            y = sbuf(f"y{hf}", [P, TILES, HALF], F32)
            for t in range(TILES):
                nc.scalar.activation(at_n5[hf][:, t, :], st[t][:].indirect(half_of(n5_t, hf)), COPY)
                nc.vector.scalar_tensor_tensor(y[:, t, :], h2[t][:, cols], -0.5, at_n5[hf][:, t, :], ALU.mult, ALU.add)
                if t % 2 == 1:
                    nc.sync.dma_start(out_rows[:, t - 1 : t + 1, cols], y[:, t - 1 : t + 1, :])
            y_half = sbuf(f"y_half{hf}", [P, HALF * 4], BF16)
            nc.vector.tensor_copy(
                y_half[:].rearrange("p (c i t) -> p c t i", i=4, t=TILES), y[:].rearrange("p t (c i) -> p c t i", i=4)
            )
            nc.vector.quantize_mx(out=y_codes[:, cols].bitcast(FP8X4), scales=y_plane[:, cols], in_=y_half[:])
            nc.sync.dma_start(out_words[:, cols], y_codes[:, cols].bitcast(I32))
        for q in range(4):
            queue = nc.sync if q % 2 == 0 else nc.scalar
            queue.dma_start(out_2[0, 4 * q : 4 * q + 4, :].bitcast(I32), y_plane[32 * q : 32 * q + 4, :].bitcast(I32))
